import numpy as np
import ml_dtypes


def mxq(x, axis, fmt="e4m3"):
    dtype, down = {"e4m3": (ml_dtypes.float8_e4m3fn, 7), "e5m2": (ml_dtypes.float8_e5m2, 14)}[fmt]
    v = np.moveaxis(np.asarray(x, np.float32).astype(ml_dtypes.bfloat16).astype(np.float64), axis, -1)
    blocks = v.reshape(v.shape[:-1] + (-1, 32))
    amax = np.abs(blocks).max(-1, keepdims=True)
    byte = np.maximum(np.where(amax > 0, np.frexp(amax)[1] - 1 + 127, 0) - down, 1)
    scale = np.exp2(byte - 127.0)
    codes = (blocks / scale).astype(np.float32).astype(dtype).astype(np.float64)
    return np.moveaxis((codes * scale).reshape(v.shape), -1, axis)


WIDE = False


def mx_kscale(k):
    if not WIDE:
        return np.ones(k)
    levels = np.array([10, -10, 5, -5, 0])
    if k % 512:
        return np.exp2(np.random.permutation(np.resize(levels, k // 32))).repeat(32)
    a = np.empty((k // 512, 16))
    for p in range(k // 512):
        a[p, :8] = np.random.permutation(np.resize(levels, 8))
        for g in range(8):
            far = levels[np.abs(levels - a[p, g]) >= 10]
            a[p, g + 8] = far[np.random.randint(len(far))]
    return np.exp2(a.ravel()).repeat(32)


BF16 = ml_dtypes.bfloat16


def bf(x):
    return np.asarray(x, np.float32).astype(BF16)


def f64(x):
    return np.asarray(x).astype(np.float64)


E2M1 = np.array([0.0, 0.5, 1.0, 1.5, 2.0, 3.0, 4.0, 6.0, -0.0, -0.5, -1.0, -1.5, -2.0, -3.0, -4.0, -6.0])


def pack_weight(w, fmt):
    k, n = w.shape
    w = f64(bf(w)).reshape(k // 32, 32, n)
    amax = np.abs(w).max(1)
    if fmt == "e4m3":
        byte = np.frexp(amax)[1] - 1 + 127 - 7
    else:
        mant, ex = np.frexp(amax / 6.0)
        byte = np.where(mant > 0.5, ex, ex - 1) + 127
    byte = np.clip(np.where(amax > 0, byte, 1), 1, 254)
    scaled = (w * np.exp2(127.0 - byte)[:, None, :]).reshape(k, n).astype(np.float32)
    by_word = np.ascontiguousarray(scaled.reshape(k // 512, 128, 4, n).transpose(0, 1, 3, 2))
    if fmt == "e4m3":
        words = by_word.astype(ml_dtypes.float8_e4m3fn).view(np.uint8)
    else:
        c = by_word.astype(ml_dtypes.float4_e2m1fn).view(np.uint8) & 0xF
        words = c[..., 0::2] | (c[..., 1::2] << 4)
    return np.ascontiguousarray(words), np.ascontiguousarray(byte.astype(np.uint8).reshape(k // 512, 16, n))


def unpack_weight(words, scales, fmt):
    g, p, n, _ = words.shape
    if fmt == "e4m3":
        vals = np.ascontiguousarray(words).view(ml_dtypes.float8_e4m3fn).astype(np.float64)
    else:
        nib = np.empty((g, p, n, 4), np.uint8)
        nib[..., 0::2] = words & 0xF
        nib[..., 1::2] = words >> 4
        vals = E2M1[nib]
    vals = vals * np.repeat(np.exp2(scales.astype(np.float64) - 127.0), 8, axis=1)[..., None]
    return vals.transpose(0, 1, 3, 2).reshape(g * 512, n)
def pack4(w):
    words, scales = pack_weight(w, "e2m1")
    return words.reshape(words.shape[0], 128, -1), scales


def unpack4(words, scales):
    return unpack_weight(words.reshape(words.shape[0], 128, -1, 2), scales, "e2m1")


T, A, F, D = 1024, 1024, 3072, 1024


def setup_inputs():
    s = mx_kscale(A)
    t = mx_kscale(F)
    attn = np.random.standard_normal((T, A)) * s
    wo = np.random.standard_normal((A, D)) / np.sqrt(A) / s[:, None]
    up = np.random.standard_normal((T, F)) * t
    wd = np.random.standard_normal((F, D)) / np.sqrt(F) / t[:, None]
    wd_words, wd_scales = pack4(wd)
    return {"attn": bf(attn),
            "wo": bf(wo),
            "gate": bf(np.random.standard_normal((T, F))),
            "up": bf(up),
            "wd_words": wd_words,
            "wd_scales": wd_scales,
            "gain": bf(1 + 0.1 * np.random.standard_normal(D)),
            "resid": bf(np.random.standard_normal((T, D)))}


def reference(attn, wo, gate, up, wd_words, wd_scales, gain, resid):
    h = np.maximum(f64(gate), 0.0) * f64(up)
    from_attn = mxq(f64(attn), 1, "e4m3") @ mxq(f64(wo), 0, "e4m3")
    from_mlp = mxq(h, 1, "e4m3") @ unpack4(wd_words, wd_scales)
    both = from_attn + from_mlp
    return f64(resid) + both * f64(gain)

@@ -1,0 +1,401 @@
+from contextlib import ExitStack
+
+import concourse.mybir as mybir
+from concourse.masks import make_identity
+
+T, A, F, D = 1024, 1024, 3072, 1024
+FLOPS = 2 * T * (A + F) * D
+
+F32 = mybir.dt.float32
+BF16 = mybir.dt.bfloat16
+I32 = mybir.dt.int32
+U32 = mybir.dt.uint32
+U8 = mybir.dt.uint8
+FP8X4 = mybir.dt.float8_e4m3fn_x4
+FP4X4 = mybir.dt.float4_e2m1fn_x4
+ALU = mybir.AluOpType
+ACT = mybir.ActivationFunctionType
+
+P = 128
+PACK = 4
+K_PASS = P * PACK
+N_HALF = 512
+CHUNK = 2 * K_PASS
+TILES = T // P
+MLP_CHUNKS = F // CHUNK
+ATTN = MLP_CHUNKS
+
+HEAD_TILES = 3
+ADD_FROM = [0, 2, 5, 8, 12, 14]
+WO_STEPS = [[8,2,"i",0,0],[9,0,"i",0,1],[9,0,"q",0,0],[9,0,"i",1,0],[9,0,"q",0,1],[9,1,"i",1,1],[9,1,"q",1,0],[10,1,"q",1,1]]
+WO_AT = [9, 9]
+SORT_FROM = 4
+S_RELU_FROM = 9
+HELD = 2
+RESID_LAG = 2
+WO_VECTOR_COLS = 320
+STREAM_BUFS = 6
+SORT_H = True
+V_RELU = 1
+
+
+def tile_parallel_block_output_s1_kernel(tc, attn, wo, gate, up, wd_words, wd_scales, gain, resid, out):
+    nc = tc.nc
+    with ExitStack() as ctx:
+        keep = ctx.enter_context(tc.tile_pool(name="keep", bufs=1))
+        work = ctx.enter_context(tc.tile_pool(name="work", bufs=1))
+        psum = ctx.enter_context(tc.psum_pool(name="psum", bufs=1))
+        ctx.enter_context(tc.manual_schedule())
+
+        ident = keep.tile([P, P], F32, name="ident")
+        wd_sc = keep.tile([P, F // K_PASS, D], U8, name="wd_sc", align_bytes=64)
+        gain_raw = keep.tile([P, D // P], BF16, name="gain_raw")
+        gain_f32 = keep.tile([P, D // P], F32, name="gain_f32")
+        gain_all = keep.tile([P, D], F32, name="gain_all")
+        warm = keep.tile([P, 8], BF16, name="warm")
+
+        gate_sb, up_sb, attn_sb, resid_sb, wd_sb, wo_sb = {}, {}, {}, {}, {}, {}
+        hidden, turned, grouped, codes, scales, acc, result = {}, {}, {}, {}, {}, {}, {}
+        wo_grouped, wo_codes, wo_scales = {}, {}, {}
+
+        def rows(t):
+            return slice(t * P, (t + 1) * P)
+
+        def cols(c):
+            return slice(c * CHUNK, (c + 1) * CHUNK)
+
+        def half(h):
+            return slice(h * N_HALF, (h + 1) * N_HALF)
+
+        def bank(b, shape):
+            return psum.tile(shape, F32, name="bank%d" % b, tag="bank%d" % b)
+
+        def load_gate(t, c=None):
+            if t not in gate_sb:
+                gate_sb[t] = work.tile([P, F], BF16, name="gate_sb", tag="gate_sb", bufs=STREAM_BUFS)
+            if c is None:
+                nc.sync.dma_start(out=gate_sb[t][:], in_=gate[rows(t), :])
+            else:
+                nc.sync.dma_start(out=gate_sb[t][:, cols(c)], in_=gate[rows(t), cols(c)])
+
+        def load_up(t, c):
+            up_sb[t, c] = work.tile([P, CHUNK], BF16, name="up_sb", tag="up_sb", bufs=STREAM_BUFS * MLP_CHUNKS)
+            nc.sync.dma_start(out=up_sb[t, c][:], in_=up[rows(t), cols(c)])
+
+        def load_attn(t):
+            attn_sb[t] = work.tile([P, A], BF16, name="attn_sb", tag="attn_sb", bufs=TILES)
+            nc.sync.dma_start(out=attn_sb[t][:], in_=attn[rows(t), :])
+
+        def load_resid(t):
+            resid_sb[t] = work.tile([P, D], BF16, name="resid_sb", tag="resid_sb", bufs=TILES)
+            nc.sync.dma_start(out=resid_sb[t][:], in_=resid[rows(t), :])
+
+        def load_wd(c):
+            wd_sb[c] = work.tile([P, 2, 2 * D], U8, name="wd_sb", tag="wd_sb", bufs=MLP_CHUNKS, align_bytes=64)
+            nc.sync.dma_start(
+                out=wd_sb[c][:].bitcast(I32),
+                in_=wd_words[2 * c : 2 * c + 2].rearrange("g p b -> p g b").bitcast(I32),
+            )
+
+        def load_wd_scales():
+            for q in range(4):
+                nc.sync.dma_start(
+                    out=wd_sc[32 * q : 32 * q + 4].bitcast(I32),
+                    in_=wd_scales[:, 4 * q : 4 * q + 4, :].rearrange("g r n -> r g n").bitcast(I32),
+                )
+
+        def load_wo(g):
+            wo_sb[g] = work.tile([P, PACK, D], BF16, name="wo_sb", tag="wo_sb", bufs=2)
+            nc.sync.dma_start(
+                out=wo_sb[g][:], in_=wo[g * K_PASS : (g + 1) * K_PASS, :].rearrange("(p j) n -> p j n", j=PACK)
+            )
+
+        def load_tile(t):
+            load_attn(t)
+            load_gate(t)
+            for c in range(MLP_CHUNKS):
+                load_up(t, c)
+
+        def relu(t, c, on_vector):
+            g = gate_sb[t][:, cols(c)]
+            if on_vector:
+                nc.vector.tensor_scalar_max(out=g, in0=g, scalar1=0.0)
+            else:
+                nc.scalar.activation(out=g, in_=g, func=ACT.Relu)
+
+        def product(t, c):
+            hidden[t, c] = work.tile([P, CHUNK], BF16, name="hidden", tag="hidden", bufs=6)
+            if SORT_H:
+                nc.vector.tensor_tensor(
+                    out=hidden[t, c][:].rearrange("p (u w e) -> p u w e", u=2, e=2),
+                    in0=gate_sb[t][:, cols(c)].rearrange("p (w u e) -> p u w e", u=2, e=2),
+                    in1=up_sb[t, c][:].rearrange("p (w u e) -> p u w e", u=2, e=2),
+                    op=ALU.mult,
+                )
+            else:
+                nc.vector.tensor_tensor(out=hidden[t, c][:], in0=gate_sb[t][:, cols(c)], in1=up_sb[t, c][:], op=ALU.mult)
+
+        def sort_attn(t):
+            hidden[t, ATTN] = work.tile([P, CHUNK], BF16, name="hidden", tag="hidden", bufs=6)
+            nc.scalar.copy(
+                out=hidden[t, ATTN][:].bitcast(F32).rearrange("p (u w) -> p u w", u=2),
+                in_=attn_sb[t][:].bitcast(F32).rearrange("p (w u) -> p u w", u=2),
+            )
+
+        def turn(t, c, b):
+            turned[t, c] = bank(b, [P, 2, 2, P])
+            is_sorted = t >= SORT_FROM if c == ATTN else SORT_H
+            src = hidden[t, c] if (c != ATTN or is_sorted) else attn_sb[t]
+            words = src[:].bitcast(F32)
+            for g in range(2):
+                for u in range(2):
+                    if is_sorted:
+                        w = words[:, 2 * P * u + P * g : 2 * P * u + P * (g + 1)]
+                    else:
+                        w = words[:, 2 * P * g + u : 2 * P * (g + 1) : 2]
+                    nc.tensor.transpose(turned[t, c][:, g, u, :], w, ident[:])
+
+        def copy_out(t, c):
+            grouped[t, c] = work.tile([P, CHUNK], BF16, name="grouped", tag="grouped", bufs=4, align_bytes=64)
+            nc.scalar.copy(
+                out=grouped[t, c][:].bitcast(F32).rearrange("p (g r u) -> p g r u", g=2, u=2),
+                in_=turned[t, c][:].rearrange("p g u r -> p g r u"),
+            )
+
+        def quantize(t, c):
+            codes[t, c] = work.tile([P, 2 * P], U32, name="codes", tag="codes", bufs=8, align_bytes=64)
+            scales[t, c] = work.tile([P, 2 * P], U8, name="scales", tag="scales", bufs=8, align_bytes=64)
+            nc.vector.quantize_mx(out=codes[t, c][:].bitcast(FP8X4), scales=scales[t, c][:], in_=grouped[t, c][:])
+
+        def wo_interleave(g, h):
+            wo_grouped[g, h] = work.tile([P, N_HALF, PACK], BF16, name="wo_grouped", tag="wo_grouped", bufs=2, align_bytes=64)
+            src = wo_sb[g][:, :, half(h)].rearrange("p j n -> p n j")
+            v = WO_VECTOR_COLS
+            nc.scalar.copy(out=wo_grouped[g, h][:, v:, :], in_=src[:, v:, :])
+            nc.vector.tensor_copy(out=wo_grouped[g, h][:, :v, :], in_=src[:, :v, :])
+
+        def wo_quantize(g, h):
+            wo_codes[g, h] = work.tile([P, N_HALF], U32, name="wo_codes", tag="wo_codes", bufs=4, align_bytes=64)
+            wo_scales[g, h] = work.tile([P, N_HALF], U8, name="wo_scales", tag="wo_scales", bufs=4, align_bytes=64)
+            nc.vector.quantize_mx(
+                out=wo_codes[g, h][:].bitcast(FP8X4),
+                scales=wo_scales[g, h][:],
+                in_=wo_grouped[g, h][:].rearrange("p n j -> p (n j)"),
+            )
+
+        def multiply(t, h, c, g, start, stop):
+            if start:
+                acc[t, h] = bank(acc_bank(t) + h, [P, N_HALF])
+            if c == ATTN:
+                rhs, rhs_scale = wo_codes[g, h][:].bitcast(FP8X4), wo_scales[g, h][:]
+            else:
+                rhs = wd_sb[c][:, g, 2 * N_HALF * h : 2 * N_HALF * (h + 1)].bitcast(FP4X4)
+                rhs_scale = wd_sc[:, 2 * c + g, half(h)]
+            nc.tensor.matmul_mx(
+                out=acc[t, h][:],
+                lhsT=codes[t, c][:, g * P : (g + 1) * P].bitcast(FP8X4),
+                lhsT_scale=scales[t, c][:, g * P : (g + 1) * P],
+                rhs=rhs,
+                rhs_scale=rhs_scale,
+                start=start,
+                stop=stop,
+            )
+
+        def acc_bank(t):
+            return 2 * t if t < HEAD_TILES else 2 + 2 * ((t - HEAD_TILES) % 2)
+
+        def apply_gain(t, h, lo=0, hi=N_HALF):
+            if t not in result:
+                result[t] = work.tile([P, D], F32, name="result", tag="result", bufs=TILES)
+            c = slice(h * N_HALF + lo, h * N_HALF + hi)
+            nc.vector.tensor_tensor(out=result[t][:, c], in0=acc[t, h][:, lo:hi], in1=gain_all[:, c], op=ALU.mult)
+
+        def add_resid(t, h, lo=0, hi=N_HALF):
+            c = slice(h * N_HALF + lo, h * N_HALF + hi)
+            nc.vector.tensor_tensor(out=result[t][:, c], in0=result[t][:, c], in1=resid_sb[t][:, c], op=ALU.add)
+
+        def store(t, lo=0, hi=D):
+            nc.sync.dma_start(out=out[rows(t), lo:hi], in_=result[t][:, lo:hi])
+
+        nc.vector.memset(wd_sc[:].rearrange("p g n -> p (g n)").bitcast(I32), 0)
+        nc.vector.memset(warm[:], 0.0)
+        nc.scalar.activation(out=warm[:], in_=warm[:], func=ACT.Relu)
+        make_identity(nc, ident[:])
+
+        units = [(t, c) for c in range(MLP_CHUNKS + 1) for t in range(HEAD_TILES)]
+        for n, (t, c) in enumerate(units):
+            for g in range(2):
+                if n == WO_AT[g]:
+                    load_wo(g)
+            if c == ATTN:
+                load_attn(t)
+            else:
+                load_gate(t, c)
+                load_up(t, c)
+                if n == 0:
+                    nc.sync.dma_start(out=gain_raw[:], in_=gain.rearrange("(p c) -> p c", p=P))
+                    load_wd_scales()
+                if t == 0:
+                    load_wd(c)
+        for t in range(HEAD_TILES, STREAM_BUFS):
+            load_tile(t)
+            if t >= RESID_LAG:
+                for r in range(t - RESID_LAG + 1):
+                    if r not in resid_sb:
+                        load_resid(r)
+
+        def spread_gain():
+            nc.vector.tensor_copy(out=gain_f32[:], in_=gain_raw[:])
+            for b in range(2):
+                spread = bank(4 + b, [P, 4, P])
+                for j in range(4):
+                    c = 4 * b + j
+                    nc.tensor.transpose(spread[:, j, :], gain_f32[:, c : c + 1].to_broadcast([P, P]), ident[:])
+                nc.scalar.copy(
+                    out=gain_all[:].rearrange("q (p c) -> q p c", p=P)[:, :, 4 * b : 4 * b + 4],
+                    in_=spread[:].rearrange("q j p -> q p j"),
+                )
+
+        def wo_work(n, where):
+            for step, place, what, x, y in WO_STEPS:
+                if step == n and place == where:
+                    if what == "i":
+                        wo_interleave(x, y)
+                    else:
+                        wo_quantize(x, y)
+
+        def head_relu(n):
+            if n < len(units) and units[n][1] != ATTN:
+                relu(*units[n], n < S_RELU_FROM)
+
+        def unit_multiply(n):
+            t, c = units[n]
+            for g in range(2):
+                for h in range(2):
+                    multiply(t, h, c, g, c == 0 and g == 0, c == ATTN and g == 1)
+
+        head_relu(0)
+        product(*units[0])
+        turn(*units[0], 6)
+        copy_out(*units[0])
+        spread_gain()
+        quantize(*units[0])
+        unit_multiply(0)
+        head_relu(1)
+        n_mlp = HEAD_TILES * MLP_CHUNKS
+        for n in range(1, n_mlp):
+            wo_work(n, 0)
+            product(*units[n])
+            turn(*units[n], 6 + n % 2)
+            copy_out(*units[n])
+            head_relu(n + 1)
+            wo_work(n, 1)
+            if n > 1:
+                quantize(*units[n - 1])
+                unit_multiply(n - 1)
+            wo_work(n, 2)
+        for t in range(STREAM_BUFS, TILES):
+            load_tile(t)
+            load_resid(t - RESID_LAG)
+        for t in range(TILES - RESID_LAG, TILES):
+            load_resid(t)
+        quantize(*units[n_mlp - 1])
+        wo_work(n_mlp, 0)
+        unit_multiply(n_mlp - 1)
+        for t in range(HEAD_TILES):
+            if t >= SORT_FROM:
+                sort_attn(t)
+            turn(t, ATTN, 6 + (n_mlp + t) % 2)
+            copy_out(t, ATTN)
+            wo_work(n_mlp + t, 1)
+            quantize(t, ATTN)
+            wo_work(n_mlp + t, 2)
+        t3 = HEAD_TILES
+        unit_multiply(n_mlp)
+        if t3 >= SORT_FROM:
+            sort_attn(t3)
+        relu(t3, 0, True)
+        relu(t3, 1, False)
+        turn(t3, ATTN, 6)
+        copy_out(t3, ATTN)
+        relu(t3, 2, False)
+        apply_gain(0, 0)
+        apply_gain(0, 1)
+        product(t3, 0)
+        unit_multiply(n_mlp + 1)
+        product(t3, 1)
+        quantize(t3, ATTN)
+        product(t3, 2)
+
+        order = [ATTN] + list(range(MLP_CHUNKS))
+        passes = [(c, g) for c in order for g in range(2)]
+        turn_banks = [6, 7, 0, 1]
+        adds = [(a, h) for a in range(TILES - 1) for h in range(2)]
+        for t in range(HEAD_TILES, TILES):
+            nxt = t + 1 if t + 1 < TILES else None
+            first = t == HEAD_TILES
+            for i, c in enumerate(order):
+                if not (first and i == 0):
+                    turn(t, c, turn_banks[i])
+                    copy_out(t, c)
+            if first:
+                unit_multiply(n_mlp + 2)
+                apply_gain(1, 0)
+                apply_gain(1, 1)
+            else:
+                for c, g in passes[len(passes) - HELD :]:
+                    multiply(t - 1, 1, c, g, False, (c, g) == passes[-1])
+                quantize(t, order[0])
+            mine = adds[ADD_FROM[t - HEAD_TILES] : ADD_FROM[t - HEAD_TILES + 1]]
+            if nxt is not None and not first:
+                for c in range(V_RELU):
+                    relu(nxt, c, True)
+            quantize(t, order[1])
+            quantize(t, order[2])
+            if first:
+                apply_gain(t - 1, 0)
+            else:
+                apply_gain(t - 1, 1)
+            quantize(t, order[3])
+            if first:
+                apply_gain(t - 1, 1)
+                for c in range(V_RELU):
+                    relu(nxt, c, True)
+            if nxt is not None:
+                if nxt >= SORT_FROM:
+                    sort_attn(nxt)
+                for c in range(V_RELU, MLP_CHUNKS):
+                    relu(nxt, c, False)
+            for i, (c, g) in enumerate(passes):
+                multiply(t, 0, c, g, i == 0, i == len(passes) - 1)
+            held = HELD if nxt is not None else 0
+            for i, (c, g) in enumerate(passes[: len(passes) - held]):
+                multiply(t, 1, c, g, i == 0, i == len(passes) - 1)
+            if nxt is not None:
+                product(nxt, 0)
+                for a, h in mine[:1]:
+                    add_resid(a, h)
+                product(nxt, 1)
+                for a, h in mine[1:2]:
+                    add_resid(a, h)
+                product(nxt, 2)
+                apply_gain(t, 0)
+                for a, h in mine[2:]:
+                    add_resid(a, h)
+            else:
+                for a, h in mine:
+                    add_resid(a, h)
+            for a, h in mine:
+                if h == 1:
+                    store(a)
+        t = TILES - 1
+        q = N_HALF // 2
+        apply_gain(t, 0)
+        add_resid(t, 0)
+        store(t, 0, N_HALF)
+        apply_gain(t, 1, 0, q)
+        apply_gain(t, 1, q, N_HALF)
+        add_resid(t, 1, 0, q)
+        add_resid(t, 1, q, N_HALF)
+        store(t, N_HALF, N_HALF + q)
+        store(t, N_HALF + q, D)

@@ -25,18 +25,21 @@ TILES = T // P
 MLP_CHUNKS = F // CHUNK
 ATTN = MLP_CHUNKS
 
-HEAD_TILES = 3
-ADD_FROM = [0, 2, 5, 8, 12, 14]
-WO_STEPS = [[8,2,"i",0,0],[9,0,"i",0,1],[9,0,"q",0,0],[9,0,"i",1,0],[9,0,"q",0,1],[9,1,"i",1,1],[9,1,"q",1,0],[10,1,"q",1,1]]
-WO_AT = [9, 9]
-SORT_FROM = 4
-S_RELU_FROM = 9
-HELD = 2
+HEAD_TILES = 2
 RESID_LAG = 2
 WO_VECTOR_COLS = 320
 STREAM_BUFS = 6
-SORT_H = True
+SORT_WRITE = False
+SORT_FROM = 4
 V_RELU = 1
+HEAD_V_RELU = True
+SCALES_AT = 2
+ADD_FROM = [0, 1, 2, 3, 4, 6, 7]
+PAIR_FROM = 9
+HALF_MAJOR_FROM = 7
+JOIN_P = 0
+ADD_FIRST = False
+WHOLE_UP_FROM = 4
 
 
 def tile_parallel_block_output_s1_kernel(tc, attn, wo, gate, up, wd_words, wd_scales, gain, resid, out):
@@ -61,8 +64,8 @@ def tile_parallel_block_output_s1_kernel(tc, attn, wo, gate, up, wd_words, wd_sc
         def rows(t):
             return slice(t * P, (t + 1) * P)
 
-        def cols(c):
-            return slice(c * CHUNK, (c + 1) * CHUNK)
+        def cols(c, n=1):
+            return slice(c * CHUNK, (c + n) * CHUNK)
 
         def half(h):
             return slice(h * N_HALF, (h + 1) * N_HALF)
@@ -78,9 +81,10 @@ def tile_parallel_block_output_s1_kernel(tc, attn, wo, gate, up, wd_words, wd_sc
             else:
                 nc.sync.dma_start(out=gate_sb[t][:, cols(c)], in_=gate[rows(t), cols(c)])
 
-        def load_up(t, c):
-            up_sb[t, c] = work.tile([P, CHUNK], BF16, name="up_sb", tag="up_sb", bufs=STREAM_BUFS * MLP_CHUNKS)
-            nc.sync.dma_start(out=up_sb[t, c][:], in_=up[rows(t), cols(c)])
+        def load_up(t, c, n=1):
+            if t not in up_sb:
+                up_sb[t] = work.tile([P, F], BF16, name="up_sb", tag="up_sb", bufs=STREAM_BUFS)
+            nc.sync.dma_start(out=up_sb[t][:, cols(c, n)], in_=up[rows(t), cols(c, n)])
 
         def load_attn(t):
             attn_sb[t] = work.tile([P, A], BF16, name="attn_sb", tag="attn_sb", bufs=TILES)
@@ -111,64 +115,78 @@ def tile_parallel_block_output_s1_kernel(tc, attn, wo, gate, up, wd_words, wd_sc
             )
 
         def load_tile(t):
-            load_attn(t)
             load_gate(t)
-            for c in range(MLP_CHUNKS):
-                load_up(t, c)
+            if t >= WHOLE_UP_FROM:
+                load_up(t, 0, MLP_CHUNKS)
+            else:
+                for c in range(MLP_CHUNKS):
+                    load_up(t, c)
+            if t + 1 < TILES:
+                load_attn(t + 1)
 
-        def relu(t, c, on_vector):
-            g = gate_sb[t][:, cols(c)]
+        def relu(t, c, on_vector, n=1):
+            g = gate_sb[t][:, cols(c, n)]
             if on_vector:
                 nc.vector.tensor_scalar_max(out=g, in0=g, scalar1=0.0)
             else:
                 nc.scalar.activation(out=g, in_=g, func=ACT.Relu)
 
-        def product(t, c):
-            hidden[t, c] = work.tile([P, CHUNK], BF16, name="hidden", tag="hidden", bufs=6)
-            if SORT_H:
-                nc.vector.tensor_tensor(
-                    out=hidden[t, c][:].rearrange("p (u w e) -> p u w e", u=2, e=2),
-                    in0=gate_sb[t][:, cols(c)].rearrange("p (w u e) -> p u w e", u=2, e=2),
-                    in1=up_sb[t, c][:].rearrange("p (w u e) -> p u w e", u=2, e=2),
-                    op=ALU.mult,
-                )
-            else:
-                nc.vector.tensor_tensor(out=hidden[t, c][:], in0=gate_sb[t][:, cols(c)], in1=up_sb[t, c][:], op=ALU.mult)
+        def product(t, c, n=1):
+            h = work.tile([P, n * CHUNK], BF16, name="hidden", tag="hidden%d" % n, bufs=4 if n == 1 else 2)
+            for i in range(n):
+                hidden[t, c + i] = (h, n, i)
+            order = "p w u e" if SORT_WRITE else "p u w e"
+            nc.vector.tensor_tensor(
+                out=h[:].rearrange("p (u w e) -> " + order, u=2, e=2),
+                in0=gate_sb[t][:, cols(c, n)].rearrange("p (w u e) -> " + order, u=2, e=2),
+                in1=up_sb[t][:, cols(c, n)].rearrange("p (w u e) -> " + order, u=2, e=2),
+                op=ALU.mult,
+            )
 
         def sort_attn(t):
-            hidden[t, ATTN] = work.tile([P, CHUNK], BF16, name="hidden", tag="hidden", bufs=6)
+            h = work.tile([P, CHUNK], BF16, name="hidden", tag="hidden1", bufs=4)
+            hidden[t, ATTN] = (h, 1, 0)
             nc.scalar.copy(
-                out=hidden[t, ATTN][:].bitcast(F32).rearrange("p (u w) -> p u w", u=2),
+                out=h[:].bitcast(F32).rearrange("p (u w) -> p u w", u=2),
                 in_=attn_sb[t][:].bitcast(F32).rearrange("p (w u) -> p u w", u=2),
             )
 
         def turn(t, c, b):
             turned[t, c] = bank(b, [P, 2, 2, P])
-            is_sorted = t >= SORT_FROM if c == ATTN else SORT_H
-            src = hidden[t, c] if (c != ATTN or is_sorted) else attn_sb[t]
-            words = src[:].bitcast(F32)
             for g in range(2):
                 for u in range(2):
-                    if is_sorted:
-                        w = words[:, 2 * P * u + P * g : 2 * P * u + P * (g + 1)]
+                    if (t, c) in hidden:
+                        h, n, i = hidden[t, c]
+                        w0 = 2 * P * n * u + 2 * P * i + P * g
+                        w = h[:].bitcast(F32)[:, w0 : w0 + P]
                     else:
-                        w = words[:, 2 * P * g + u : 2 * P * (g + 1) : 2]
+                        w = attn_sb[t][:].bitcast(F32)[:, 2 * P * g + u : 2 * P * (g + 1) : 2]
                     nc.tensor.transpose(turned[t, c][:, g, u, :], w, ident[:])
 
-        def copy_out(t, c):
-            grouped[t, c] = work.tile([P, CHUNK], BF16, name="grouped", tag="grouped", bufs=4, align_bytes=64)
+        def copy_out(t, c, join=None, n=1):
+            if join is None:
+                grouped[t, c] = (work.tile([P, n * CHUNK], BF16, name="grouped", tag="grouped%d" % n, bufs=4 if n == 1 else 2, align_bytes=64), 0, [(t, c)])
+            else:
+                grouped[t, c] = (grouped[join][0], 1, None)
+                grouped[join][2].append((t, c))
+            dst, i, members = grouped[t, c]
             nc.scalar.copy(
-                out=grouped[t, c][:].bitcast(F32).rearrange("p (g r u) -> p g r u", g=2, u=2),
+                out=dst[:, cols(i)].bitcast(F32).rearrange("p (g r u) -> p g r u", g=2, u=2),
                 in_=turned[t, c][:].rearrange("p g u r -> p g r u"),
             )
 
         def quantize(t, c):
-            codes[t, c] = work.tile([P, 2 * P], U32, name="codes", tag="codes", bufs=8, align_bytes=64)
-            scales[t, c] = work.tile([P, 2 * P], U8, name="scales", tag="scales", bufs=8, align_bytes=64)
-            nc.vector.quantize_mx(out=codes[t, c][:].bitcast(FP8X4), scales=scales[t, c][:], in_=grouped[t, c][:])
+            src, i, members = grouped[t, c]
+            n = len(members)
+            cw = work.tile([P, n * 2 * P], U32, name="codes", tag="codes%d" % n, bufs=5 if n == 1 else 4, align_bytes=64)
+            sc = work.tile([P, n * 2 * P], U8, name="scales", tag="scales%d" % n, bufs=5 if n == 1 else 4, align_bytes=64)
+            nc.vector.quantize_mx(out=cw[:].bitcast(FP8X4), scales=sc[:], in_=src[:])
+            for i, key in enumerate(members):
+                codes[key] = cw[:, i * 2 * P : (i + 1) * 2 * P]
+                scales[key] = sc[:, i * 2 * P : (i + 1) * 2 * P]
 
         def wo_interleave(g, h):
-            wo_grouped[g, h] = work.tile([P, N_HALF, PACK], BF16, name="wo_grouped", tag="wo_grouped", bufs=2, align_bytes=64)
+            wo_grouped[g, h] = work.tile([P, N_HALF, PACK], BF16, name="wo_grouped", tag="grouped2", bufs=2, align_bytes=64)
             src = wo_sb[g][:, :, half(h)].rearrange("p j n -> p n j")
             v = WO_VECTOR_COLS
             nc.scalar.copy(out=wo_grouped[g, h][:, v:, :], in_=src[:, v:, :])
@@ -202,7 +220,7 @@ def tile_parallel_block_output_s1_kernel(tc, attn, wo, gate, up, wd_words, wd_sc
             )
 
         def acc_bank(t):
-            return 2 * t if t < HEAD_TILES else 2 + 2 * ((t - HEAD_TILES) % 2)
+            return 2 * (t % 2)
 
         def apply_gain(t, h, lo=0, hi=N_HALF):
             if t not in result:
@@ -210,8 +228,8 @@ def tile_parallel_block_output_s1_kernel(tc, attn, wo, gate, up, wd_words, wd_sc
             c = slice(h * N_HALF + lo, h * N_HALF + hi)
             nc.vector.tensor_tensor(out=result[t][:, c], in0=acc[t, h][:, lo:hi], in1=gain_all[:, c], op=ALU.mult)
 
-        def add_resid(t, h, lo=0, hi=N_HALF):
-            c = slice(h * N_HALF + lo, h * N_HALF + hi)
+        def add_resid(t, lo=0, hi=D):
+            c = slice(lo, hi)
             nc.vector.tensor_tensor(out=result[t][:, c], in0=result[t][:, c], in1=resid_sb[t][:, c], op=ALU.add)
 
         def store(t, lo=0, hi=D):
@@ -222,32 +240,37 @@ def tile_parallel_block_output_s1_kernel(tc, attn, wo, gate, up, wd_words, wd_sc
         nc.scalar.activation(out=warm[:], in_=warm[:], func=ACT.Relu)
         make_identity(nc, ident[:])
 
-        units = [(t, c) for c in range(MLP_CHUNKS + 1) for t in range(HEAD_TILES)]
-        for n, (t, c) in enumerate(units):
-            for g in range(2):
-                if n == WO_AT[g]:
-                    load_wo(g)
-            if c == ATTN:
-                load_attn(t)
-            else:
-                load_gate(t, c)
-                load_up(t, c)
-                if n == 0:
-                    nc.sync.dma_start(out=gain_raw[:], in_=gain.rearrange("(p c) -> p c", p=P))
-                    load_wd_scales()
-                if t == 0:
-                    load_wd(c)
+        def load_small():
+            load_wd_scales()
+
+        load_attn(0)
+        nc.sync.dma_start(out=gain_raw[:], in_=gain.rearrange("(p c) -> p c", p=P))
+        if SCALES_AT == 0:
+            load_small()
+        load_wo(0)
+        if SCALES_AT == 1:
+            load_small()
+        load_attn(1)
+        load_wo(1)
+        if SCALES_AT == 2:
+            load_small()
+        units = [(t, c) for c in range(MLP_CHUNKS) for t in range(HEAD_TILES)]
+        for t, c in units:
+            load_gate(t, c)
+            load_up(t, c)
+            if t == 0:
+                load_wd(c)
+        load_attn(HEAD_TILES)
         for t in range(HEAD_TILES, STREAM_BUFS):
             load_tile(t)
-            if t >= RESID_LAG:
-                for r in range(t - RESID_LAG + 1):
-                    if r not in resid_sb:
-                        load_resid(r)
+            for r in range(t - RESID_LAG + 1):
+                if r not in resid_sb:
+                    load_resid(r)
 
         def spread_gain():
             nc.vector.tensor_copy(out=gain_f32[:], in_=gain_raw[:])
             for b in range(2):
-                spread = bank(4 + b, [P, 4, P])
+                spread = bank(6 + b, [P, 4, P])
                 for j in range(4):
                     c = 4 * b + j
                     nc.tensor.transpose(spread[:, j, :], gain_f32[:, c : c + 1].to_broadcast([P, P]), ident[:])
@@ -256,146 +279,136 @@ def tile_parallel_block_output_s1_kernel(tc, attn, wo, gate, up, wd_words, wd_sc
                     in_=spread[:].rearrange("q j p -> q p j"),
                 )
 
-        def wo_work(n, where):
-            for step, place, what, x, y in WO_STEPS:
-                if step == n and place == where:
-                    if what == "i":
-                        wo_interleave(x, y)
-                    else:
-                        wo_quantize(x, y)
+        def turn_attn(t, b):
+            if t >= SORT_FROM:
+                sort_attn(t)
+            turn(t, ATTN, b)
+            copy_out(t, ATTN)
 
-        def head_relu(n):
-            if n < len(units) and units[n][1] != ATTN:
-                relu(*units[n], n < S_RELU_FROM)
+        turn_attn(0, 4)
+        spread_gain()
+        quantize(0, ATTN)
+        wo_interleave(0, 0)
+        wo_interleave(0, 1)
+        turn_attn(1, 5)
+        wo_quantize(0, 0)
+        wo_quantize(0, 1)
+        quantize(1, ATTN)
+        wo_interleave(1, 0)
+        wo_interleave(1, 1)
+        wo_quantize(1, 0)
+        wo_quantize(1, 1)
+        for g in range(2):
+            for h in range(2):
+                for t in range(HEAD_TILES):
+                    multiply(t, h, ATTN, g, g == 0, False)
 
         def unit_multiply(n):
             t, c = units[n]
-            for g in range(2):
-                for h in range(2):
-                    multiply(t, h, c, g, c == 0 and g == 0, c == ATTN and g == 1)
+            for h in range(2):
+                for g in range(2):
+                    multiply(t, h, c, g, False, c == MLP_CHUNKS - 1 and g == 1)
 
-        head_relu(0)
-        product(*units[0])
-        turn(*units[0], 6)
-        copy_out(*units[0])
-        spread_gain()
-        quantize(*units[0])
-        unit_multiply(0)
-        head_relu(1)
-        n_mlp = HEAD_TILES * MLP_CHUNKS
-        for n in range(1, n_mlp):
-            wo_work(n, 0)
-            product(*units[n])
-            turn(*units[n], 6 + n % 2)
-            copy_out(*units[n])
-            head_relu(n + 1)
-            wo_work(n, 1)
-            if n > 1:
+        for n, (t, c) in enumerate(units):
+            relu(t, c, HEAD_V_RELU)
+            product(t, c)
+            turn(t, c, 4 + n % 4)
+            copy_out(t, c)
+            if n > 0:
                 quantize(*units[n - 1])
                 unit_multiply(n - 1)
-            wo_work(n, 2)
         for t in range(STREAM_BUFS, TILES):
             load_tile(t)
             load_resid(t - RESID_LAG)
         for t in range(TILES - RESID_LAG, TILES):
             load_resid(t)
-        quantize(*units[n_mlp - 1])
-        wo_work(n_mlp, 0)
-        unit_multiply(n_mlp - 1)
-        for t in range(HEAD_TILES):
-            if t >= SORT_FROM:
-                sort_attn(t)
-            turn(t, ATTN, 6 + (n_mlp + t) % 2)
-            copy_out(t, ATTN)
-            wo_work(n_mlp + t, 1)
-            quantize(t, ATTN)
-            wo_work(n_mlp + t, 2)
-        t3 = HEAD_TILES
-        unit_multiply(n_mlp)
-        if t3 >= SORT_FROM:
-            sort_attn(t3)
-        relu(t3, 0, True)
-        relu(t3, 1, False)
-        turn(t3, ATTN, 6)
-        copy_out(t3, ATTN)
-        relu(t3, 2, False)
+        t2 = HEAD_TILES
+        relu(t2, 2, False)
+        turn_attn(t2, 6)
+        quantize(*units[-1])
+        unit_multiply(len(units) - 1)
+        relu(t2, 0, True, 2)
+        product(t2, 0)
+        product(t2, 1)
+        product(t2, 2)
         apply_gain(0, 0)
+        quantize(t2, ATTN)
         apply_gain(0, 1)
-        product(t3, 0)
-        unit_multiply(n_mlp + 1)
-        product(t3, 1)
-        quantize(t3, ATTN)
-        product(t3, 2)
 
-        order = [ATTN] + list(range(MLP_CHUNKS))
-        passes = [(c, g) for c in order for g in range(2)]
-        turn_banks = [6, 7, 0, 1]
-        adds = [(a, h) for a in range(TILES - 1) for h in range(2)]
+        q = N_HALF // 2
         for t in range(HEAD_TILES, TILES):
             nxt = t + 1 if t + 1 < TILES else None
-            first = t == HEAD_TILES
-            for i, c in enumerate(order):
-                if not (first and i == 0):
-                    turn(t, c, turn_banks[i])
-                    copy_out(t, c)
-            if first:
-                unit_multiply(n_mlp + 2)
-                apply_gain(1, 0)
-                apply_gain(1, 1)
-            else:
-                for c, g in passes[len(passes) - HELD :]:
-                    multiply(t - 1, 1, c, g, False, (c, g) == passes[-1])
-                quantize(t, order[0])
-            mine = adds[ADD_FROM[t - HEAD_TILES] : ADD_FROM[t - HEAD_TILES + 1]]
-            if nxt is not None and not first:
-                for c in range(V_RELU):
-                    relu(nxt, c, True)
-            quantize(t, order[1])
-            quantize(t, order[2])
-            if first:
-                apply_gain(t - 1, 0)
-            else:
-                apply_gain(t - 1, 1)
-            quantize(t, order[3])
-            if first:
-                apply_gain(t - 1, 1)
-                for c in range(V_RELU):
-                    relu(nxt, c, True)
+            mine = list(range(ADD_FROM[t - HEAD_TILES], ADD_FROM[t - HEAD_TILES + 1]))
+            if nxt is not None and nxt >= SORT_FROM and t == HEAD_TILES:
+                sort_attn(nxt)
+            pair = t >= PAIR_FROM
+            turn(t, 0, 4)
+            copy_out(t, 0, n=2 if pair else 1)
+            turn(t, 1, 5)
+            copy_out(t, 1, join=(t, 0) if pair else None)
+            turn(t, 2, 6)
+            copy_out(t, 2, n=2 if pair and nxt is not None else 1)
             if nxt is not None:
-                if nxt >= SORT_FROM:
-                    sort_attn(nxt)
-                for c in range(V_RELU, MLP_CHUNKS):
-                    relu(nxt, c, False)
-            for i, (c, g) in enumerate(passes):
-                multiply(t, 0, c, g, i == 0, i == len(passes) - 1)
-            held = HELD if nxt is not None else 0
-            for i, (c, g) in enumerate(passes[: len(passes) - held]):
-                multiply(t, 1, c, g, i == 0, i == len(passes) - 1)
+                turn(nxt, ATTN, 7)
+                copy_out(nxt, ATTN, join=(t, 2) if pair else None)
+            for h in range(2):
+                for g in range(2):
+                    multiply(t, h, ATTN, g, g == 0, False)
+            if t > HEAD_TILES:
+                apply_gain(t - 1, 1)
+                if nxt is not None:
+                    for c in range(V_RELU):
+                        relu(nxt, c, True)
+            quantize(t, 0)
+            if not pair:
+                quantize(t, 1)
+            if t == HEAD_TILES:
+                apply_gain(t - 1, 0)
+                quantize(t, 2)
+                for c in range(V_RELU):
+                    relu(nxt, c, True)
+                apply_gain(t - 1, 1)
             if nxt is not None:
                 product(nxt, 0)
-                for a, h in mine[:1]:
-                    add_resid(a, h)
-                product(nxt, 1)
-                for a, h in mine[1:2]:
-                    add_resid(a, h)
-                product(nxt, 2)
+            if t > HEAD_TILES:
+                quantize(t, 2)
+            if not ADD_FIRST:
+                for a in mine[:1]:
+                    add_resid(a)
+            if nxt is not None:
+                if JOIN_P and t >= JOIN_P:
+                    relu(nxt, 1, False, 2)
+                else:
+                    for c in range(V_RELU, MLP_CHUNKS):
+                        relu(nxt, c, False)
+                if nxt + 1 < TILES and nxt + 1 >= SORT_FROM:
+                    sort_attn(nxt + 1)
+            seq = [(0, 0), (0, 1), (1, 0), (2, 0), (1, 1), (2, 1)]
+            if t >= HALF_MAJOR_FROM:
+                seq = [(c, h) for h in range(2) for c in range(MLP_CHUNKS)]
+            for c, h in seq:
+                for g in range(2):
+                    multiply(t, h, c, g, False, c == MLP_CHUNKS - 1 and g == 1)
+            if nxt is not None:
+                if not pair:
+                    quantize(nxt, ATTN)
+                if JOIN_P and t >= JOIN_P:
+                    product(nxt, 1, 2)
+                else:
+                    product(nxt, 1)
+                    product(nxt, 2)
                 apply_gain(t, 0)
-                for a, h in mine[2:]:
-                    add_resid(a, h)
-            else:
-                for a, h in mine:
-                    add_resid(a, h)
-            for a, h in mine:
-                if h == 1:
-                    store(a)
+            for a in mine[1:]:
+                add_resid(a)
+            for a in mine:
+                store(a)
         t = TILES - 1
-        q = N_HALF // 2
         apply_gain(t, 0)
-        add_resid(t, 0)
+        add_resid(t, 0, N_HALF)
         store(t, 0, N_HALF)
         apply_gain(t, 1, 0, q)
         apply_gain(t, 1, q, N_HALF)
-        add_resid(t, 1, 0, q)
-        add_resid(t, 1, q, N_HALF)
+        add_resid(t, N_HALF, N_HALF + q)
+        add_resid(t, N_HALF + q, D)
         store(t, N_HALF, N_HALF + q)
         store(t, N_HALF + q, D)

@@ -29,7 +29,7 @@ HEAD_TILES = 2
 RESID_LAG = 2
 WO_VECTOR_COLS = 320
 STREAM_BUFS = 6
-SORT_WRITE = False
+SORT_WRITE = True
 SORT_FROM = 4
 V_RELU = 1
 HEAD_V_RELU = True

@@ -24,22 +24,13 @@ CHUNK = 2 * K_PASS
 TILES = T // P
 MLP_CHUNKS = F // CHUNK
 ATTN = MLP_CHUNKS
+TURN_BANK = 4
 
 HEAD_TILES = 2
+STREAM_BUFS = 6
 RESID_LAG = 2
 WO_VECTOR_COLS = 320
-STREAM_BUFS = 6
-SORT_WRITE = True
-SORT_FROM = 4
-V_RELU = 1
-HEAD_V_RELU = True
-SCALES_AT = 2
-ADD_FROM = [0, 1, 2, 3, 4, 6, 7]
-PAIR_FROM = 9
-HALF_MAJOR_FROM = 7
-JOIN_P = 0
-ADD_FIRST = False
-WHOLE_UP_FROM = 4
+CHUNKED_UP_TILES = 4
 
 
 def tile_parallel_block_output_s1_kernel(tc, attn, wo, gate, up, wd_words, wd_scales, gain, resid, out):
@@ -55,10 +46,9 @@ def tile_parallel_block_output_s1_kernel(tc, attn, wo, gate, up, wd_words, wd_sc
         gain_raw = keep.tile([P, D // P], BF16, name="gain_raw")
         gain_f32 = keep.tile([P, D // P], F32, name="gain_f32")
         gain_all = keep.tile([P, D], F32, name="gain_all")
-        warm = keep.tile([P, 8], BF16, name="warm")
 
         gate_sb, up_sb, attn_sb, resid_sb, wd_sb, wo_sb = {}, {}, {}, {}, {}, {}
-        hidden, turned, grouped, codes, scales, acc, result = {}, {}, {}, {}, {}, {}, {}
+        sorted_sb, turned, grouped, codes, scales, acc, result = {}, {}, {}, {}, {}, {}, {}
         wo_grouped, wo_codes, wo_scales = {}, {}, {}
 
         def rows(t):
@@ -73,29 +63,26 @@ def tile_parallel_block_output_s1_kernel(tc, attn, wo, gate, up, wd_words, wd_sc
         def bank(b, shape):
             return psum.tile(shape, F32, name="bank%d" % b, tag="bank%d" % b)
 
-        def load_gate(t, c=None):
+        def load_gate(t, c, n=1):
             if t not in gate_sb:
-                gate_sb[t] = work.tile([P, F], BF16, name="gate_sb", tag="gate_sb", bufs=STREAM_BUFS)
-            if c is None:
-                nc.sync.dma_start(out=gate_sb[t][:], in_=gate[rows(t), :])
-            else:
-                nc.sync.dma_start(out=gate_sb[t][:, cols(c)], in_=gate[rows(t), cols(c)])
+                gate_sb[t] = work.tile([P, F], BF16, name="gate_sb", bufs=STREAM_BUFS)
+            nc.sync.dma_start(out=gate_sb[t][:, cols(c, n)], in_=gate[rows(t), cols(c, n)])
 
         def load_up(t, c, n=1):
             if t not in up_sb:
-                up_sb[t] = work.tile([P, F], BF16, name="up_sb", tag="up_sb", bufs=STREAM_BUFS)
+                up_sb[t] = work.tile([P, F], BF16, name="up_sb", bufs=STREAM_BUFS)
             nc.sync.dma_start(out=up_sb[t][:, cols(c, n)], in_=up[rows(t), cols(c, n)])
 
         def load_attn(t):
-            attn_sb[t] = work.tile([P, A], BF16, name="attn_sb", tag="attn_sb", bufs=TILES)
+            attn_sb[t] = work.tile([P, A], BF16, name="attn_sb", bufs=TILES)
             nc.sync.dma_start(out=attn_sb[t][:], in_=attn[rows(t), :])
 
         def load_resid(t):
-            resid_sb[t] = work.tile([P, D], BF16, name="resid_sb", tag="resid_sb", bufs=TILES)
+            resid_sb[t] = work.tile([P, D], BF16, name="resid_sb", bufs=TILES)
             nc.sync.dma_start(out=resid_sb[t][:], in_=resid[rows(t), :])
 
         def load_wd(c):
-            wd_sb[c] = work.tile([P, 2, 2 * D], U8, name="wd_sb", tag="wd_sb", bufs=MLP_CHUNKS, align_bytes=64)
+            wd_sb[c] = work.tile([P, 2, 2 * D], U8, name="wd_sb", bufs=MLP_CHUNKS, align_bytes=64)
             nc.sync.dma_start(
                 out=wd_sb[c][:].bitcast(I32),
                 in_=wd_words[2 * c : 2 * c + 2].rearrange("g p b -> p g b").bitcast(I32),
@@ -109,45 +96,43 @@ def tile_parallel_block_output_s1_kernel(tc, attn, wo, gate, up, wd_words, wd_sc
                 )
 
         def load_wo(g):
-            wo_sb[g] = work.tile([P, PACK, D], BF16, name="wo_sb", tag="wo_sb", bufs=2)
+            wo_sb[g] = work.tile([P, PACK, D], BF16, name="wo_sb", bufs=A // K_PASS)
             nc.sync.dma_start(
                 out=wo_sb[g][:], in_=wo[g * K_PASS : (g + 1) * K_PASS, :].rearrange("(p j) n -> p j n", j=PACK)
             )
 
         def load_tile(t):
-            load_gate(t)
-            if t >= WHOLE_UP_FROM:
-                load_up(t, 0, MLP_CHUNKS)
-            else:
+            load_gate(t, 0, MLP_CHUNKS)
+            if t < CHUNKED_UP_TILES:
                 for c in range(MLP_CHUNKS):
                     load_up(t, c)
+            else:
+                load_up(t, 0, MLP_CHUNKS)
             if t + 1 < TILES:
                 load_attn(t + 1)
+            load_resid(t - RESID_LAG)
 
-        def relu(t, c, on_vector, n=1):
+        def relu_on_vector(t, c, n=1):
             g = gate_sb[t][:, cols(c, n)]
-            if on_vector:
-                nc.vector.tensor_scalar_max(out=g, in0=g, scalar1=0.0)
-            else:
-                nc.scalar.activation(out=g, in_=g, func=ACT.Relu)
+            nc.vector.tensor_scalar_max(out=g, in0=g, scalar1=0.0)
 
-        def product(t, c, n=1):
-            h = work.tile([P, n * CHUNK], BF16, name="hidden", tag="hidden%d" % n, bufs=4 if n == 1 else 2)
-            for i in range(n):
-                hidden[t, c + i] = (h, n, i)
-            order = "p w u e" if SORT_WRITE else "p u w e"
+        def relu_on_scalar(t, c):
+            g = gate_sb[t][:, cols(c)]
+            nc.scalar.activation(out=g, in_=g, func=ACT.Relu)
+
+        def product(t, c):
+            sorted_sb[t, c] = work.tile([P, CHUNK], BF16, name="sorted_sb", bufs=4)
             nc.vector.tensor_tensor(
-                out=h[:].rearrange("p (u w e) -> " + order, u=2, e=2),
-                in0=gate_sb[t][:, cols(c, n)].rearrange("p (w u e) -> " + order, u=2, e=2),
-                in1=up_sb[t][:, cols(c, n)].rearrange("p (w u e) -> " + order, u=2, e=2),
+                out=sorted_sb[t, c][:].rearrange("p (u w e) -> p w u e", u=2, e=2),
+                in0=gate_sb[t][:, cols(c)].rearrange("p (w u e) -> p w u e", u=2, e=2),
+                in1=up_sb[t][:, cols(c)].rearrange("p (w u e) -> p w u e", u=2, e=2),
                 op=ALU.mult,
             )
 
         def sort_attn(t):
-            h = work.tile([P, CHUNK], BF16, name="hidden", tag="hidden1", bufs=4)
-            hidden[t, ATTN] = (h, 1, 0)
+            sorted_sb[t, ATTN] = work.tile([P, CHUNK], BF16, name="sorted_sb", bufs=4)
             nc.scalar.copy(
-                out=h[:].bitcast(F32).rearrange("p (u w) -> p u w", u=2),
+                out=sorted_sb[t, ATTN][:].bitcast(F32).rearrange("p (u w) -> p u w", u=2),
                 in_=attn_sb[t][:].bitcast(F32).rearrange("p (w u) -> p u w", u=2),
             )
 
@@ -155,55 +140,42 @@ def tile_parallel_block_output_s1_kernel(tc, attn, wo, gate, up, wd_words, wd_sc
             turned[t, c] = bank(b, [P, 2, 2, P])
             for g in range(2):
                 for u in range(2):
-                    if (t, c) in hidden:
-                        h, n, i = hidden[t, c]
-                        w0 = 2 * P * n * u + 2 * P * i + P * g
-                        w = h[:].bitcast(F32)[:, w0 : w0 + P]
+                    if (t, c) in sorted_sb:
+                        first = 2 * P * u + P * g
+                        pairs = sorted_sb[t, c][:].bitcast(F32)[:, first : first + P]
                     else:
-                        w = attn_sb[t][:].bitcast(F32)[:, 2 * P * g + u : 2 * P * (g + 1) : 2]
-                    nc.tensor.transpose(turned[t, c][:, g, u, :], w, ident[:])
-
-        def copy_out(t, c, join=None, n=1):
-            if join is None:
-                grouped[t, c] = (work.tile([P, n * CHUNK], BF16, name="grouped", tag="grouped%d" % n, bufs=4 if n == 1 else 2, align_bytes=64), 0, [(t, c)])
-            else:
-                grouped[t, c] = (grouped[join][0], 1, None)
-                grouped[join][2].append((t, c))
-            dst, i, members = grouped[t, c]
+                        pairs = attn_sb[t][:].bitcast(F32)[:, 2 * P * g + u : 2 * P * (g + 1) : 2]
+                    nc.tensor.transpose(turned[t, c][:, g, u, :], pairs, ident[:])
+            grouped[t, c] = work.tile([P, CHUNK], BF16, name="grouped", bufs=4, align_bytes=64)
             nc.scalar.copy(
-                out=dst[:, cols(i)].bitcast(F32).rearrange("p (g r u) -> p g r u", g=2, u=2),
+                out=grouped[t, c][:].bitcast(F32).rearrange("p (g r u) -> p g r u", g=2, u=2),
                 in_=turned[t, c][:].rearrange("p g u r -> p g r u"),
             )
 
         def quantize(t, c):
-            src, i, members = grouped[t, c]
-            n = len(members)
-            cw = work.tile([P, n * 2 * P], U32, name="codes", tag="codes%d" % n, bufs=5 if n == 1 else 4, align_bytes=64)
-            sc = work.tile([P, n * 2 * P], U8, name="scales", tag="scales%d" % n, bufs=5 if n == 1 else 4, align_bytes=64)
-            nc.vector.quantize_mx(out=cw[:].bitcast(FP8X4), scales=sc[:], in_=src[:])
-            for i, key in enumerate(members):
-                codes[key] = cw[:, i * 2 * P : (i + 1) * 2 * P]
-                scales[key] = sc[:, i * 2 * P : (i + 1) * 2 * P]
+            codes[t, c] = work.tile([P, 2 * P], U32, name="codes", bufs=5, align_bytes=64)
+            scales[t, c] = work.tile([P, 2 * P], U8, name="scales", bufs=5, align_bytes=64)
+            nc.vector.quantize_mx(out=codes[t, c][:].bitcast(FP8X4), scales=scales[t, c][:], in_=grouped[t, c][:])
 
         def wo_interleave(g, h):
-            wo_grouped[g, h] = work.tile([P, N_HALF, PACK], BF16, name="wo_grouped", tag="grouped2", bufs=2, align_bytes=64)
+            wo_grouped[g, h] = work.tile([P, N_HALF, PACK], BF16, name="wo_grouped", bufs=2, align_bytes=64)
             src = wo_sb[g][:, :, half(h)].rearrange("p j n -> p n j")
-            v = WO_VECTOR_COLS
-            nc.scalar.copy(out=wo_grouped[g, h][:, v:, :], in_=src[:, v:, :])
-            nc.vector.tensor_copy(out=wo_grouped[g, h][:, :v, :], in_=src[:, :v, :])
+            nc.scalar.copy(out=wo_grouped[g, h][:, WO_VECTOR_COLS:, :], in_=src[:, WO_VECTOR_COLS:, :])
+            nc.vector.tensor_copy(out=wo_grouped[g, h][:, :WO_VECTOR_COLS, :], in_=src[:, :WO_VECTOR_COLS, :])
 
         def wo_quantize(g, h):
-            wo_codes[g, h] = work.tile([P, N_HALF], U32, name="wo_codes", tag="wo_codes", bufs=4, align_bytes=64)
-            wo_scales[g, h] = work.tile([P, N_HALF], U8, name="wo_scales", tag="wo_scales", bufs=4, align_bytes=64)
+            wo_codes[g, h] = work.tile([P, N_HALF], U32, name="wo_codes", bufs=4, align_bytes=64)
+            wo_scales[g, h] = work.tile([P, N_HALF], U8, name="wo_scales", bufs=4, align_bytes=64)
             nc.vector.quantize_mx(
                 out=wo_codes[g, h][:].bitcast(FP8X4),
                 scales=wo_scales[g, h][:],
                 in_=wo_grouped[g, h][:].rearrange("p n j -> p (n j)"),
             )
 
-        def multiply(t, h, c, g, start, stop):
+        def multiply(t, h, c, g):
+            start = c == ATTN and g == 0
             if start:
-                acc[t, h] = bank(acc_bank(t) + h, [P, N_HALF])
+                acc[t, h] = bank(2 * (t % 2) + h, [P, N_HALF])
             if c == ATTN:
                 rhs, rhs_scale = wo_codes[g, h][:].bitcast(FP8X4), wo_scales[g, h][:]
             else:
@@ -216,61 +188,31 @@ def tile_parallel_block_output_s1_kernel(tc, attn, wo, gate, up, wd_words, wd_sc
                 rhs=rhs,
                 rhs_scale=rhs_scale,
                 start=start,
-                stop=stop,
+                stop=c == MLP_CHUNKS - 1 and g == 1,
             )
 
-        def acc_bank(t):
-            return 2 * (t % 2)
+        def multiply_chunk(t, c, halves=(0, 1)):
+            for h in halves:
+                for g in range(2):
+                    multiply(t, h, c, g)
 
         def apply_gain(t, h, lo=0, hi=N_HALF):
             if t not in result:
-                result[t] = work.tile([P, D], F32, name="result", tag="result", bufs=TILES)
-            c = slice(h * N_HALF + lo, h * N_HALF + hi)
-            nc.vector.tensor_tensor(out=result[t][:, c], in0=acc[t, h][:, lo:hi], in1=gain_all[:, c], op=ALU.mult)
+                result[t] = work.tile([P, D], F32, name="result", bufs=TILES)
+            ch = slice(h * N_HALF + lo, h * N_HALF + hi)
+            nc.vector.tensor_tensor(out=result[t][:, ch], in0=acc[t, h][:, lo:hi], in1=gain_all[:, ch], op=ALU.mult)
 
         def add_resid(t, lo=0, hi=D):
-            c = slice(lo, hi)
-            nc.vector.tensor_tensor(out=result[t][:, c], in0=result[t][:, c], in1=resid_sb[t][:, c], op=ALU.add)
+            nc.vector.tensor_tensor(
+                out=result[t][:, lo:hi], in0=result[t][:, lo:hi], in1=resid_sb[t][:, lo:hi], op=ALU.add
+            )
 
         def store(t, lo=0, hi=D):
             nc.sync.dma_start(out=out[rows(t), lo:hi], in_=result[t][:, lo:hi])
 
-        nc.vector.memset(wd_sc[:].rearrange("p g n -> p (g n)").bitcast(I32), 0)
-        nc.vector.memset(warm[:], 0.0)
-        nc.scalar.activation(out=warm[:], in_=warm[:], func=ACT.Relu)
-        make_identity(nc, ident[:])
-
-        def load_small():
-            load_wd_scales()
-
-        load_attn(0)
-        nc.sync.dma_start(out=gain_raw[:], in_=gain.rearrange("(p c) -> p c", p=P))
-        if SCALES_AT == 0:
-            load_small()
-        load_wo(0)
-        if SCALES_AT == 1:
-            load_small()
-        load_attn(1)
-        load_wo(1)
-        if SCALES_AT == 2:
-            load_small()
-        units = [(t, c) for c in range(MLP_CHUNKS) for t in range(HEAD_TILES)]
-        for t, c in units:
-            load_gate(t, c)
-            load_up(t, c)
-            if t == 0:
-                load_wd(c)
-        load_attn(HEAD_TILES)
-        for t in range(HEAD_TILES, STREAM_BUFS):
-            load_tile(t)
-            for r in range(t - RESID_LAG + 1):
-                if r not in resid_sb:
-                    load_resid(r)
-
         def spread_gain():
-            nc.vector.tensor_copy(out=gain_f32[:], in_=gain_raw[:])
             for b in range(2):
-                spread = bank(6 + b, [P, 4, P])
+                spread = bank(TURN_BANK + 2 + b, [P, 4, P])
                 for j in range(4):
                     c = 4 * b + j
                     nc.tensor.transpose(spread[:, j, :], gain_f32[:, c : c + 1].to_broadcast([P, P]), ident[:])
@@ -279,136 +221,118 @@ def tile_parallel_block_output_s1_kernel(tc, attn, wo, gate, up, wd_words, wd_sc
                     in_=spread[:].rearrange("q j p -> q p j"),
                 )
 
-        def turn_attn(t, b):
-            if t >= SORT_FROM:
-                sort_attn(t)
-            turn(t, ATTN, b)
-            copy_out(t, ATTN)
+        nc.vector.memset(wd_sc[:].rearrange("p g n -> p (g n)").bitcast(I32), 0)
+        make_identity(nc, ident[:])
 
-        turn_attn(0, 4)
-        spread_gain()
+        head = [(0, 0), (1, 0)] + [(t, c) for t in range(HEAD_TILES) for c in range(1, MLP_CHUNKS)]
+        nc.sync.dma_start(out=gain_raw[:], in_=gain.rearrange("(p c) -> p c", p=P))
+        for g in range(2):
+            load_attn(g)
+            load_wo(g)
+        load_wd_scales()
+        for t, c in head:
+            load_gate(t, c)
+            load_up(t, c)
+            if t == 0:
+                load_wd(c)
+        load_attn(HEAD_TILES)
+        for t in range(HEAD_TILES, STREAM_BUFS):
+            load_tile(t)
+
+        nc.scalar.activation(out=gain_f32[:], in_=gain_raw[:], func=ACT.Copy)
+        turn(0, ATTN, TURN_BANK)
+        for h in range(2):
+            wo_interleave(0, h)
         quantize(0, ATTN)
-        wo_interleave(0, 0)
-        wo_interleave(0, 1)
-        turn_attn(1, 5)
-        wo_quantize(0, 0)
-        wo_quantize(0, 1)
+        turn(1, ATTN, TURN_BANK + 1)
+        for h in range(2):
+            wo_quantize(0, h)
+        for h in range(2):
+            wo_interleave(1, h)
         quantize(1, ATTN)
-        wo_interleave(1, 0)
-        wo_interleave(1, 1)
-        wo_quantize(1, 0)
-        wo_quantize(1, 1)
+        for h in range(2):
+            wo_quantize(1, h)
+        spread_gain()
         for g in range(2):
             for h in range(2):
                 for t in range(HEAD_TILES):
-                    multiply(t, h, ATTN, g, g == 0, False)
+                    multiply(t, h, ATTN, g)
 
-        def unit_multiply(n):
-            t, c = units[n]
-            for h in range(2):
-                for g in range(2):
-                    multiply(t, h, c, g, False, c == MLP_CHUNKS - 1 and g == 1)
-
-        for n, (t, c) in enumerate(units):
-            relu(t, c, HEAD_V_RELU)
+        for n, (t, c) in enumerate(head):
+            relu_on_vector(t, c)
             product(t, c)
-            turn(t, c, 4 + n % 4)
-            copy_out(t, c)
+            turn(t, c, TURN_BANK + n % 4)
             if n > 0:
-                quantize(*units[n - 1])
-                unit_multiply(n - 1)
+                quantize(*head[n - 1])
+                multiply_chunk(*head[n - 1])
+
         for t in range(STREAM_BUFS, TILES):
             load_tile(t)
-            load_resid(t - RESID_LAG)
         for t in range(TILES - RESID_LAG, TILES):
             load_resid(t)
-        t2 = HEAD_TILES
-        relu(t2, 2, False)
-        turn_attn(t2, 6)
-        quantize(*units[-1])
-        unit_multiply(len(units) - 1)
-        relu(t2, 0, True, 2)
-        product(t2, 0)
-        product(t2, 1)
-        product(t2, 2)
-        apply_gain(0, 0)
-        quantize(t2, ATTN)
-        apply_gain(0, 1)
 
-        q = N_HALF // 2
-        for t in range(HEAD_TILES, TILES):
-            nxt = t + 1 if t + 1 < TILES else None
-            mine = list(range(ADD_FROM[t - HEAD_TILES], ADD_FROM[t - HEAD_TILES + 1]))
-            if nxt is not None and nxt >= SORT_FROM and t == HEAD_TILES:
-                sort_attn(nxt)
-            pair = t >= PAIR_FROM
-            turn(t, 0, 4)
-            copy_out(t, 0, n=2 if pair else 1)
-            turn(t, 1, 5)
-            copy_out(t, 1, join=(t, 0) if pair else None)
-            turn(t, 2, 6)
-            copy_out(t, 2, n=2 if pair and nxt is not None else 1)
-            if nxt is not None:
-                turn(nxt, ATTN, 7)
-                copy_out(nxt, ATTN, join=(t, 2) if pair else None)
-            for h in range(2):
-                for g in range(2):
-                    multiply(t, h, ATTN, g, g == 0, False)
-            if t > HEAD_TILES:
-                apply_gain(t - 1, 1)
-                if nxt is not None:
-                    for c in range(V_RELU):
-                        relu(nxt, c, True)
+        t = HEAD_TILES
+        for h in range(2):
+            apply_gain(0, h)
+        relu_on_scalar(t, 2)
+        turn(t, ATTN, TURN_BANK + 2)
+        quantize(*head[-1])
+        multiply_chunk(*head[-1])
+        relu_on_vector(t, 0, 2)
+        for c in range(MLP_CHUNKS):
+            product(t, c)
+        quantize(t, ATTN)
+        apply_gain(1, 0)
+        sort_attn(t + 1)
+
+        for t in range(HEAD_TILES, TILES - 1):
+            for c in range(MLP_CHUNKS):
+                turn(t, c, TURN_BANK + c)
+            turn(t + 1, ATTN, TURN_BANK + ATTN)
+            multiply_chunk(t, ATTN)
+            apply_gain(t - 1, 1)
+            relu_on_vector(t + 1, 0)
             quantize(t, 0)
-            if not pair:
-                quantize(t, 1)
-            if t == HEAD_TILES:
-                apply_gain(t - 1, 0)
-                quantize(t, 2)
-                for c in range(V_RELU):
-                    relu(nxt, c, True)
-                apply_gain(t - 1, 1)
-            if nxt is not None:
-                product(nxt, 0)
-            if t > HEAD_TILES:
-                quantize(t, 2)
-            if not ADD_FIRST:
-                for a in mine[:1]:
-                    add_resid(a)
-            if nxt is not None:
-                if JOIN_P and t >= JOIN_P:
-                    relu(nxt, 1, False, 2)
-                else:
-                    for c in range(V_RELU, MLP_CHUNKS):
-                        relu(nxt, c, False)
-                if nxt + 1 < TILES and nxt + 1 >= SORT_FROM:
-                    sort_attn(nxt + 1)
-            seq = [(0, 0), (0, 1), (1, 0), (2, 0), (1, 1), (2, 1)]
-            if t >= HALF_MAJOR_FROM:
-                seq = [(c, h) for h in range(2) for c in range(MLP_CHUNKS)]
-            for c, h in seq:
-                for g in range(2):
-                    multiply(t, h, c, g, False, c == MLP_CHUNKS - 1 and g == 1)
-            if nxt is not None:
-                if not pair:
-                    quantize(nxt, ATTN)
-                if JOIN_P and t >= JOIN_P:
-                    product(nxt, 1, 2)
-                else:
-                    product(nxt, 1)
-                    product(nxt, 2)
-                apply_gain(t, 0)
-            for a in mine[1:]:
-                add_resid(a)
-            for a in mine:
-                store(a)
+            quantize(t, 1)
+            product(t + 1, 0)
+            quantize(t, 2)
+            add_resid(t - RESID_LAG)
+            relu_on_scalar(t + 1, 1)
+            relu_on_scalar(t + 1, 2)
+            if t + 2 < TILES:
+                sort_attn(t + 2)
+            multiply_chunk(t, 0)
+            for h in range(2):
+                for c in range(1, MLP_CHUNKS):
+                    multiply_chunk(t, c, (h,))
+            quantize(t + 1, ATTN)
+            product(t + 1, 1)
+            product(t + 1, 2)
+            apply_gain(t, 0)
+            store(t - RESID_LAG)
+
         t = TILES - 1
+        quarter = N_HALF // 2
+        for c in range(MLP_CHUNKS):
+            turn(t, c, TURN_BANK + c)
+        multiply_chunk(t, ATTN)
+        apply_gain(t - 1, 1)
+        add_resid(t - 2, 0, N_HALF)
+        for c in range(MLP_CHUNKS):
+            quantize(t, c)
+        add_resid(t - 2, N_HALF, D)
+        for h in range(2):
+            for c in range(MLP_CHUNKS):
+                multiply_chunk(t, c, (h,))
+        add_resid(t - 1)
+        store(t - 2)
+        store(t - 1)
         apply_gain(t, 0)
         add_resid(t, 0, N_HALF)
         store(t, 0, N_HALF)
-        apply_gain(t, 1, 0, q)
-        apply_gain(t, 1, q, N_HALF)
-        add_resid(t, N_HALF, N_HALF + q)
-        add_resid(t, N_HALF + q, D)
-        store(t, N_HALF, N_HALF + q)
-        store(t, N_HALF + q, D)
+        apply_gain(t, 1, 0, quarter)
+        apply_gain(t, 1, quarter, N_HALF)
+        add_resid(t, N_HALF, N_HALF + quarter)
+        add_resid(t, N_HALF + quarter, D)
+        store(t, N_HALF, N_HALF + quarter)
+        store(t, N_HALF + quarter, D)

from contextlib import ExitStack

import concourse.mybir as mybir
from concourse.masks import make_identity

T, A, F, D = 1024, 1024, 3072, 1024
FLOPS = 2 * T * (A + F) * D

F32 = mybir.dt.float32
BF16 = mybir.dt.bfloat16
I32 = mybir.dt.int32
U32 = mybir.dt.uint32
U8 = mybir.dt.uint8
FP8X4 = mybir.dt.float8_e4m3fn_x4
FP4X4 = mybir.dt.float4_e2m1fn_x4
ALU = mybir.AluOpType
ACT = mybir.ActivationFunctionType

P = 128
PACK = 4
K_PASS = P * PACK
N_HALF = 512
CHUNK = 2 * K_PASS
TILES = T // P
MLP_CHUNKS = F // CHUNK
ATTN = MLP_CHUNKS
TURN_BANK = 4

HEAD_TILES = 2
STREAM_BUFS = 6
RESID_LAG = 2
WO_VECTOR_COLS = 320
CHUNKED_UP_TILES = 4


def tile_parallel_block_output_s1_kernel(tc, attn, wo, gate, up, wd_words, wd_scales, gain, resid, out):
    nc = tc.nc
    with ExitStack() as ctx:
        keep = ctx.enter_context(tc.tile_pool(name="keep", bufs=1))
        work = ctx.enter_context(tc.tile_pool(name="work", bufs=1))
        psum = ctx.enter_context(tc.psum_pool(name="psum", bufs=1))
        ctx.enter_context(tc.manual_schedule())

        ident = keep.tile([P, P], F32, name="ident")
        wd_sc = keep.tile([P, F // K_PASS, D], U8, name="wd_sc", align_bytes=64)
        gain_raw = keep.tile([P, D // P], BF16, name="gain_raw")
        gain_f32 = keep.tile([P, D // P], F32, name="gain_f32")
        gain_all = keep.tile([P, D], F32, name="gain_all")

        gate_sb, up_sb, attn_sb, resid_sb, wd_sb, wo_sb = {}, {}, {}, {}, {}, {}
        sorted_sb, turned, grouped, codes, scales, acc, result = {}, {}, {}, {}, {}, {}, {}
        wo_grouped, wo_codes, wo_scales = {}, {}, {}

        def rows(t):
            return slice(t * P, (t + 1) * P)

        def cols(c, n=1):
            return slice(c * CHUNK, (c + n) * CHUNK)

        def half(h):
            return slice(h * N_HALF, (h + 1) * N_HALF)

        def bank(b, shape):
            return psum.tile(shape, F32, name="bank%d" % b, tag="bank%d" % b)

        def load_gate(t, c, n=1):
            if t not in gate_sb:
                gate_sb[t] = work.tile([P, F], BF16, name="gate_sb", bufs=STREAM_BUFS)
            nc.sync.dma_start(out=gate_sb[t][:, cols(c, n)], in_=gate[rows(t), cols(c, n)])

        def load_up(t, c, n=1):
            if t not in up_sb:
                up_sb[t] = work.tile([P, F], BF16, name="up_sb", bufs=STREAM_BUFS)
            nc.sync.dma_start(out=up_sb[t][:, cols(c, n)], in_=up[rows(t), cols(c, n)])

        def load_attn(t):
            attn_sb[t] = work.tile([P, A], BF16, name="attn_sb", bufs=TILES)
            nc.sync.dma_start(out=attn_sb[t][:], in_=attn[rows(t), :])

        def load_resid(t):
            resid_sb[t] = work.tile([P, D], BF16, name="resid_sb", bufs=TILES)
            nc.sync.dma_start(out=resid_sb[t][:], in_=resid[rows(t), :])

        def load_wd(c):
            wd_sb[c] = work.tile([P, 2, 2 * D], U8, name="wd_sb", bufs=MLP_CHUNKS, align_bytes=64)
            nc.sync.dma_start(
                out=wd_sb[c][:].bitcast(I32),
                in_=wd_words[2 * c : 2 * c + 2].rearrange("g p b -> p g b").bitcast(I32),
            )

        def load_wd_scales():
            for q in range(4):
                nc.sync.dma_start(
                    out=wd_sc[32 * q : 32 * q + 4].bitcast(I32),
                    in_=wd_scales[:, 4 * q : 4 * q + 4, :].rearrange("g r n -> r g n").bitcast(I32),
                )

        def load_wo(g):
            wo_sb[g] = work.tile([P, PACK, D], BF16, name="wo_sb", bufs=A // K_PASS)
            nc.sync.dma_start(
                out=wo_sb[g][:], in_=wo[g * K_PASS : (g + 1) * K_PASS, :].rearrange("(p j) n -> p j n", j=PACK)
            )

        def load_tile(t):
            load_gate(t, 0, MLP_CHUNKS)
            if t < CHUNKED_UP_TILES:
                for c in range(MLP_CHUNKS):
                    load_up(t, c)
            else:
                load_up(t, 0, MLP_CHUNKS)
            if t + 1 < TILES:
                load_attn(t + 1)
            load_resid(t - RESID_LAG)

        def relu_on_vector(t, c, n=1):
            g = gate_sb[t][:, cols(c, n)]
            nc.vector.tensor_scalar_max(out=g, in0=g, scalar1=0.0)

        def relu_on_scalar(t, c):
            g = gate_sb[t][:, cols(c)]
            nc.scalar.activation(out=g, in_=g, func=ACT.Relu)

        def product(t, c):
            sorted_sb[t, c] = work.tile([P, CHUNK], BF16, name="sorted_sb", bufs=4)
            nc.vector.tensor_tensor(
                out=sorted_sb[t, c][:].rearrange("p (u w e) -> p w u e", u=2, e=2),
                in0=gate_sb[t][:, cols(c)].rearrange("p (w u e) -> p w u e", u=2, e=2),
                in1=up_sb[t][:, cols(c)].rearrange("p (w u e) -> p w u e", u=2, e=2),
                op=ALU.mult,
            )

        def sort_attn(t):
            sorted_sb[t, ATTN] = work.tile([P, CHUNK], BF16, name="sorted_sb", bufs=4)
            nc.scalar.copy(
                out=sorted_sb[t, ATTN][:].bitcast(F32).rearrange("p (u w) -> p u w", u=2),
                in_=attn_sb[t][:].bitcast(F32).rearrange("p (w u) -> p u w", u=2),
            )

        def turn(t, c, b):
            turned[t, c] = bank(b, [P, 2, 2, P])
            for g in range(2):
                for u in range(2):
                    if (t, c) in sorted_sb:
                        first = 2 * P * u + P * g
                        pairs = sorted_sb[t, c][:].bitcast(F32)[:, first : first + P]
                    else:
                        pairs = attn_sb[t][:].bitcast(F32)[:, 2 * P * g + u : 2 * P * (g + 1) : 2]
                    nc.tensor.transpose(turned[t, c][:, g, u, :], pairs, ident[:])
            grouped[t, c] = work.tile([P, CHUNK], BF16, name="grouped", bufs=4, align_bytes=64)
            nc.scalar.copy(
                out=grouped[t, c][:].bitcast(F32).rearrange("p (g r u) -> p g r u", g=2, u=2),
                in_=turned[t, c][:].rearrange("p g u r -> p g r u"),
            )

        def quantize(t, c):
            codes[t, c] = work.tile([P, 2 * P], U32, name="codes", bufs=5, align_bytes=64)
            scales[t, c] = work.tile([P, 2 * P], U8, name="scales", bufs=5, align_bytes=64)
            nc.vector.quantize_mx(out=codes[t, c][:].bitcast(FP8X4), scales=scales[t, c][:], in_=grouped[t, c][:])

        def wo_interleave(g, h):
            wo_grouped[g, h] = work.tile([P, N_HALF, PACK], BF16, name="wo_grouped", bufs=2, align_bytes=64)
            src = wo_sb[g][:, :, half(h)].rearrange("p j n -> p n j")
            nc.scalar.copy(out=wo_grouped[g, h][:, WO_VECTOR_COLS:, :], in_=src[:, WO_VECTOR_COLS:, :])
            nc.vector.tensor_copy(out=wo_grouped[g, h][:, :WO_VECTOR_COLS, :], in_=src[:, :WO_VECTOR_COLS, :])

        def wo_quantize(g, h):
            wo_codes[g, h] = work.tile([P, N_HALF], U32, name="wo_codes", bufs=4, align_bytes=64)
            wo_scales[g, h] = work.tile([P, N_HALF], U8, name="wo_scales", bufs=4, align_bytes=64)
            nc.vector.quantize_mx(
                out=wo_codes[g, h][:].bitcast(FP8X4),
                scales=wo_scales[g, h][:],
                in_=wo_grouped[g, h][:].rearrange("p n j -> p (n j)"),
            )

        def multiply(t, h, c, g):
            start = c == ATTN and g == 0
            if start:
                acc[t, h] = bank(2 * (t % 2) + h, [P, N_HALF])
            if c == ATTN:
                rhs, rhs_scale = wo_codes[g, h][:].bitcast(FP8X4), wo_scales[g, h][:]
            else:
                rhs = wd_sb[c][:, g, 2 * N_HALF * h : 2 * N_HALF * (h + 1)].bitcast(FP4X4)
                rhs_scale = wd_sc[:, 2 * c + g, half(h)]
            nc.tensor.matmul_mx(
                out=acc[t, h][:],
                lhsT=codes[t, c][:, g * P : (g + 1) * P].bitcast(FP8X4),
                lhsT_scale=scales[t, c][:, g * P : (g + 1) * P],
                rhs=rhs,
                rhs_scale=rhs_scale,
                start=start,
                stop=c == MLP_CHUNKS - 1 and g == 1,
            )

        def multiply_chunk(t, c, halves=(0, 1)):
            for h in halves:
                for g in range(2):
                    multiply(t, h, c, g)

        def apply_gain(t, h, lo=0, hi=N_HALF):
            if t not in result:
                result[t] = work.tile([P, D], F32, name="result", bufs=TILES)
            ch = slice(h * N_HALF + lo, h * N_HALF + hi)
            nc.vector.tensor_tensor(out=result[t][:, ch], in0=acc[t, h][:, lo:hi], in1=gain_all[:, ch], op=ALU.mult)

        def add_resid(t, lo=0, hi=D):
            nc.vector.tensor_tensor(
                out=result[t][:, lo:hi], in0=result[t][:, lo:hi], in1=resid_sb[t][:, lo:hi], op=ALU.add
            )

        def store(t, lo=0, hi=D):
            nc.sync.dma_start(out=out[rows(t), lo:hi], in_=result[t][:, lo:hi])

        def spread_gain():
            for b in range(2):
                spread = bank(TURN_BANK + 2 + b, [P, 4, P])
                for j in range(4):
                    c = 4 * b + j
                    nc.tensor.transpose(spread[:, j, :], gain_f32[:, c : c + 1].to_broadcast([P, P]), ident[:])
                nc.scalar.copy(
                    out=gain_all[:].rearrange("q (p c) -> q p c", p=P)[:, :, 4 * b : 4 * b + 4],
                    in_=spread[:].rearrange("q j p -> q p j"),
                )

        nc.vector.memset(wd_sc[:].rearrange("p g n -> p (g n)").bitcast(I32), 0)
        make_identity(nc, ident[:])

        head = [(0, 0), (1, 0)] + [(t, c) for t in range(HEAD_TILES) for c in range(1, MLP_CHUNKS)]
        nc.sync.dma_start(out=gain_raw[:], in_=gain.rearrange("(p c) -> p c", p=P))
        for g in range(2):
            load_attn(g)
            load_wo(g)
        load_wd_scales()
        for t, c in head:
            load_gate(t, c)
            load_up(t, c)
            if t == 0:
                load_wd(c)
        load_attn(HEAD_TILES)
        for t in range(HEAD_TILES, STREAM_BUFS):
            load_tile(t)

        nc.scalar.activation(out=gain_f32[:], in_=gain_raw[:], func=ACT.Copy)
        turn(0, ATTN, TURN_BANK)
        for h in range(2):
            wo_interleave(0, h)
        quantize(0, ATTN)
        turn(1, ATTN, TURN_BANK + 1)
        for h in range(2):
            wo_quantize(0, h)
        for h in range(2):
            wo_interleave(1, h)
        quantize(1, ATTN)
        for h in range(2):
            wo_quantize(1, h)
        spread_gain()
        for g in range(2):
            for h in range(2):
                for t in range(HEAD_TILES):
                    multiply(t, h, ATTN, g)

        for n, (t, c) in enumerate(head):
            relu_on_vector(t, c)
            product(t, c)
            turn(t, c, TURN_BANK + n % 4)
            if n > 0:
                quantize(*head[n - 1])
                multiply_chunk(*head[n - 1])

        for t in range(STREAM_BUFS, TILES):
            load_tile(t)
        for t in range(TILES - RESID_LAG, TILES):
            load_resid(t)

        t = HEAD_TILES
        for h in range(2):
            apply_gain(0, h)
        relu_on_scalar(t, 2)
        turn(t, ATTN, TURN_BANK + 2)
        quantize(*head[-1])
        multiply_chunk(*head[-1])
        relu_on_vector(t, 0, 2)
        for c in range(MLP_CHUNKS):
            product(t, c)
        quantize(t, ATTN)
        apply_gain(1, 0)
        sort_attn(t + 1)

        for t in range(HEAD_TILES, TILES - 1):
            for c in range(MLP_CHUNKS):
                turn(t, c, TURN_BANK + c)
            turn(t + 1, ATTN, TURN_BANK + ATTN)
            multiply_chunk(t, ATTN)
            apply_gain(t - 1, 1)
            relu_on_vector(t + 1, 0)
            quantize(t, 0)
            quantize(t, 1)
            product(t + 1, 0)
            quantize(t, 2)
            add_resid(t - RESID_LAG)
            relu_on_scalar(t + 1, 1)
            relu_on_scalar(t + 1, 2)
            if t + 2 < TILES:
                sort_attn(t + 2)
            multiply_chunk(t, 0)
            for h in range(2):
                for c in range(1, MLP_CHUNKS):
                    multiply_chunk(t, c, (h,))
            quantize(t + 1, ATTN)
            product(t + 1, 1)
            product(t + 1, 2)
            apply_gain(t, 0)
            store(t - RESID_LAG)

        t = TILES - 1
        quarter = N_HALF // 2
        for c in range(MLP_CHUNKS):
            turn(t, c, TURN_BANK + c)
        multiply_chunk(t, ATTN)
        apply_gain(t - 1, 1)
        add_resid(t - 2, 0, N_HALF)
        for c in range(MLP_CHUNKS):
            quantize(t, c)
        add_resid(t - 2, N_HALF, D)
        for h in range(2):
            for c in range(MLP_CHUNKS):
                multiply_chunk(t, c, (h,))
        add_resid(t - 1)
        store(t - 2)
        store(t - 1)
        apply_gain(t, 0)
        add_resid(t, 0, N_HALF)
        store(t, 0, N_HALF)
        apply_gain(t, 1, 0, quarter)
        apply_gain(t, 1, quarter, N_HALF)
        add_resid(t, N_HALF, N_HALF + quarter)
        add_resid(t, N_HALF + quarter, D)
        store(t, N_HALF, N_HALF + quarter)
        store(t, N_HALF + quarter, D)
